import numpy as np
import ml_dtypes


def mxq(x, axis, fmt="e4m3"):
    dtype, down = {"e4m3": (ml_dtypes.float8_e4m3fn, 7), "e5m2": (ml_dtypes.float8_e5m2, 14)}[fmt]
    v = np.moveaxis(np.asarray(x, np.float32).astype(ml_dtypes.bfloat16).astype(np.float64), axis, -1)
    blocks = v.reshape(v.shape[:-1] + (-1, 32))
    amax = np.abs(blocks).max(-1, keepdims=True)
    byte = np.maximum(np.where(amax > 0, np.frexp(amax)[1] - 1 + 127, 0) - down, 1)
    scale = np.exp2(byte - 127.0)
    codes = (blocks / scale).astype(np.float32).astype(dtype).astype(np.float64)
    return np.moveaxis((codes * scale).reshape(v.shape), -1, axis)


WIDE = False


def mx_kscale(k):
    if not WIDE:
        return np.ones(k)
    levels = np.array([10, -10, 5, -5, 0])
    if k % 512:
        return np.exp2(np.random.permutation(np.resize(levels, k // 32))).repeat(32)
    a = np.empty((k // 512, 16))
    for p in range(k // 512):
        a[p, :8] = np.random.permutation(np.resize(levels, 8))
        for g in range(8):
            far = levels[np.abs(levels - a[p, g]) >= 10]
            a[p, g + 8] = far[np.random.randint(len(far))]
    return np.exp2(a.ravel()).repeat(32)


def f64(x):
    return np.asarray(x).astype(np.float64)


def striped(idx):
    return np.tile(idx.reshape(-1, 16).T, (8, 1)).astype(np.uint16)


def unstriped(offs):
    return offs[:16].T.reshape(-1).astype(np.int64)


def gelu(v):
    return 0.5 * v * (1.0 + np.tanh(np.sqrt(2.0 / np.pi) * (v + 0.044715 * v**3)))


K, T, E, C, N = 1024, 1024, 2, 256, 512


def by_expert(wq, xq):
    return np.concatenate([wq[e].T @ xq[:, e * C:(e + 1) * C] for e in range(E)], axis=1)


def setup_inputs():
    n = np.random.standard_normal
    s = mx_kscale(K)[:, None]
    return {
        "xT": (n((K, T)) * s).astype(np.float32),
        "w": (n((E, K, N)) / np.sqrt(K) / s[None]).astype(np.float32),
        "b": (0.3 * n((N, E))).astype(np.float32),
        "gate": np.tile(np.random.uniform(0.2, 1.0, E * C), (N, 1)).astype(np.float32),
        "offs": striped(np.random.permutation(T)[:E * C]),
    }


def reference(xT, w, b, gate, offs):
    idx = unstriped(offs)
    xq = mxq(f64(xT)[:, idx], 0, "e4m3")
    y = by_expert(mxq(f64(w), 1, "e4m3"), xq)
    y = gelu(y + np.repeat(f64(b), C, axis=1))
    out = np.zeros((N, T))
    out[:, idx] = f64(gate) * y
    return out

@@ -1,0 +1,251 @@
+from contextlib import ExitStack
+
+import concourse.mybir as mybir
+
+K, T, E, C, N = 1024, 1024, 2, 256, 512
+S = E * C
+
+FLOPS = 2 * K * N * S
+BYTES = 4 * (K * S + E * K * N + N * E + S + N * T) + 2 * 128 * (S // 16)
+
+F32 = mybir.dt.float32
+BF16 = mybir.dt.bfloat16
+U32 = mybir.dt.uint32
+U16 = mybir.dt.uint16
+U8 = mybir.dt.uint8
+FP8X4 = mybir.dt.float8_e4m3fn_x4
+GELU = mybir.ActivationFunctionType.Gelu_apprx_tanh
+MULT = mybir.AluOpType.mult
+ADD = mybir.AluOpType.add
+
+P = 128
+G = K // (4 * P)
+M = N // P
+XG = 448
+XA = 768
+XAG = 336
+XBG = 112
+XBV = 0
+LAST = ((0, XA), (XA, T))
+
+PIECES = {
+    (0, 0): ((0, 128), (128, 256), (256, 384), (384, 512)),
+    (0, 1): ((0, 128), (128, 256), (256, 384), (384, 512)),
+    (1, 0): ((0, 512),),
+    (1, 1): ((0, 256), (256, 512)),
+}
+
+
+def tile_routed_moe_kernel(tc, xT, w, b, gate, offs, out):
+    nc = tc.nc
+    with ExitStack() as ctx:
+        lists = ctx.enter_context(tc.tile_pool(name="lists", bufs=1))
+        keep = ctx.enter_context(tc.tile_pool(name="keep", bufs=1))
+        psum = ctx.enter_context(tc.psum_pool(name="psum", bufs=1))
+
+        def gpsimd_copy(out, in_):
+            nc.gpsimd.tensor_scalar(out=out, in0=in_, scalar1=1.0, scalar2=0.0, op0=MULT, op1=ADD)
+
+        IL = {
+            (0, 0, 0): nc.scalar.copy,
+            (0, 0, 1): nc.scalar.copy,
+            (0, 0, 2): nc.scalar.copy,
+            (0, 0, 3): nc.scalar.copy,
+            (0, 1, 0): gpsimd_copy,
+            (0, 1, 1): gpsimd_copy,
+            (0, 1, 2): nc.scalar.copy,
+            (0, 1, 3): nc.scalar.copy,
+            (1, 0, 0): nc.scalar.copy,
+            (1, 0, 1): nc.scalar.copy,
+            (1, 0, 2): nc.scalar.copy,
+            (1, 0, 3): nc.scalar.copy,
+            (1, 1, 0): nc.scalar.copy,
+            (1, 1, 1): nc.scalar.copy,
+            (1, 1, 2): nc.scalar.copy,
+            (1, 1, 3): nc.scalar.copy,
+        }
+
+        offsets = lists.tile([P, S // 16], U16, name="offsets")
+        nc.sync.dma_start(offsets[:], offs)
+
+        bias = keep.tile([P, M, E], F32, name="bias")
+        nc.scalar.dma_start(bias[:], b.rearrange("(m p) e -> p m e", p=P))
+
+        w_view = w.rearrange("e (g p j) n -> e g p j n", p=P, j=4)
+        w_raw = {}
+
+        def load_w(e, g, i):
+            c0, c1 = PIECES[e, g][i]
+            w_raw[e, g, i] = keep.tile([P, 4, c1 - c0], F32, name="w_raw%d%d%d" % (e, g, i))
+            nc.sync.dma_start(w_raw[e, g, i][:], w_view[e, g, :, :, c0:c1])
+
+        x_view = xT.rearrange("(g p t) n -> g p t n", p=P, t=4)
+        x_raw = {}
+        x_last = {}
+
+        def load_x(g, u):
+            x_raw[g, u] = keep.tile([P, 2, T], F32, name="x_raw%d%d" % (g, u))
+            nc.sync.dma_start(x_raw[g, u][:], x_view[g, :, 2 * u : 2 * u + 2, :])
+
+        def load_x_last(h):
+            n0, n1 = LAST[h]
+            x_last[h] = keep.tile([P, 2, n1 - n0], F32, name="x_last%d" % h)
+            nc.sync.dma_start(x_last[h][:], x_view[1, :, 2:4, n0:n1])
+
+        gate_sb = keep.tile([P, S], F32, name="gate_sb")
+        load_x(0, 0)
+        load_x(0, 1)
+        load_x(1, 0)
+        load_x_last(0)
+        load_x_last(1)
+        load_w(0, 0, 0)
+        load_w(0, 1, 0)
+        load_w(0, 0, 1)
+        load_w(0, 1, 1)
+        nc.sync.dma_start(gate_sb[:], gate[0:P, :])
+        load_w(0, 0, 2)
+        load_w(0, 1, 2)
+        load_w(0, 0, 3)
+        load_w(0, 1, 3)
+        load_w(1, 0, 0)
+        load_w(1, 1, 0)
+        load_w(1, 1, 1)
+
+        warm_in = keep.tile([P, 1], F32, name="warm_in")
+        warm_out = keep.tile([P, 1], F32, name="warm_out")
+        nc.vector.memset(warm_in[:], 0.0)
+        nc.scalar.activation(out=warm_out[:], in_=warm_in[:], func=GELU)
+        window = []
+        for m in range(M):
+            window.append(keep.tile([P, T], F32, name="window%d" % m))
+            nc.vector.memset(window[m][:], 0.0)
+
+        w_grouped = {}
+        w_codes = {}
+        w_scales = {}
+        acc = {}
+        y = {}
+        for e in range(E):
+            for m in range(M):
+                w_grouped[e, m] = keep.tile([P, G, P, 4], BF16, name="w_grouped%d%d" % (e, m), align_bytes=64)
+                w_codes[e, m] = keep.tile([P, G * P], U32, name="w_codes%d%d" % (e, m), align_bytes=64)
+                w_scales[e, m] = keep.tile([P, G * P], U8, name="w_scales%d%d" % (e, m), align_bytes=64)
+                acc[e, m] = psum.tile([P, C], F32, name="acc%d%d" % (e, m))
+                y[e, m] = keep.tile([P, C], F32, name="y%d%d" % (e, m))
+
+        def interleave(e, g, m):
+            for i, (c0, c1) in enumerate(PIECES[e, g]):
+                if c0 <= m * P < c1:
+                    a = m * P - c0
+                    IL[e, g, m](
+                        out=w_grouped[e, m][:, g, :, :],
+                        in_=w_raw[e, g, i][:, :, a : a + P].rearrange("p j n -> p n j"),
+                    )
+
+        def quantize_w(e, m):
+            nc.vector.quantize_mx(
+                out=w_codes[e, m][:].bitcast(FP8X4),
+                scales=w_scales[e, m][:],
+                in_=w_grouped[e, m][:].rearrange("p g n j -> p (g n j)"),
+            )
+
+        x_grouped = {}
+        x_words = {}
+        x_codes = {}
+        x_scales = {}
+        pairs = {}
+        for g in range(G):
+            x_grouped[g] = keep.tile([P, S, 4], BF16, name="x_grouped%d" % g, align_bytes=64)
+            x_words[g] = (
+                x_grouped[g][:].rearrange("p s t -> p (s t)").bitcast(U32).rearrange("p (s u) -> p s u", u=2)
+            )
+            x_codes[g] = keep.tile([P, S], U32, name="x_codes%d" % g, align_bytes=64)
+            x_scales[g] = keep.tile([P, S], U8, name="x_scales%d" % g, align_bytes=64)
+
+        def quantize_x(g, s0, s1):
+            nc.vector.quantize_mx(
+                out=x_codes[g][:, s0:s1].bitcast(FP8X4),
+                scales=x_scales[g][:, s0:s1],
+                in_=x_grouped[g][:, s0:s1, :].rearrange("p s t -> p (s t)"),
+            )
+
+        def gather(g, u, s0, s1):
+            pair_words = pairs[g, u][:].rearrange("p n e -> p (n e)").bitcast(U32)
+            nc.vector.tensor_copy(
+                out=x_words[g][:, s0:s1, u], in_=pair_words.indirect(offsets[:, s0 // 16 : s1 // 16])
+            )
+
+        def multiply(e, g, m):
+            nc.tensor.matmul_mx(
+                out=acc[e, m][:],
+                lhsT=w_codes[e, m][:, g * P : (g + 1) * P].bitcast(FP8X4),
+                lhsT_scale=w_scales[e, m][:, g * P : (g + 1) * P],
+                rhs=x_codes[g][:, e * C : (e + 1) * C].bitcast(FP8X4),
+                rhs_scale=x_scales[g][:, e * C : (e + 1) * C],
+                start=(g == 0),
+                stop=(g == G - 1),
+            )
+
+        def activate(e, m):
+            nc.scalar.activation(
+                out=y[e, m][:], in_=acc[e, m][:], func=GELU, bias=bias[:, m, e : e + 1], scale=1.0
+            )
+
+        def scatter(e, m):
+            slot_offsets = offsets[:, e * (C // 16) : (e + 1) * (C // 16)]
+            nc.vector.tensor_tensor(
+                out=window[m][:].indirect(slot_offsets), in0=y[e, m][:], in1=gate_sb[:, e * C : (e + 1) * C], op=MULT
+            )
+
+        def cast(copy, dst, n0, raw, r0, r1):
+            if r1 > r0:
+                copy(out=dst[:, n0 + r0 : n0 + r1, :], in_=raw[:, :, r0:r1].rearrange("p e n -> p n e"))
+
+        for g, u in ((0, 0), (0, 1), (1, 0)):
+            pairs[g, u] = keep.tile([P, T, 2], BF16, name="pairs%d%d" % (g, u))
+            cast(nc.scalar.copy, pairs[g, u], 0, x_raw[g, u], 0, T - XG)
+            cast(gpsimd_copy, pairs[g, u], 0, x_raw[g, u], T - XG, T)
+            gather(g, u, 0, S)
+            if (g, u) == (0, 1):
+                quantize_x(0, 0, S)
+        pairs[1, 1] = keep.tile([P, T, 2], BF16, name="pairs11")
+        cast(nc.scalar.copy, pairs[1, 1], 0, x_last[0], 0, XA - XAG)
+        cast(gpsimd_copy, pairs[1, 1], 0, x_last[0], XA - XAG, XA)
+        cast(nc.vector.tensor_copy, pairs[1, 1], XA, x_last[1], 0, XBV)
+        cast(nc.scalar.copy, pairs[1, 1], XA, x_last[1], XBV, T - XA - XBG)
+        cast(gpsimd_copy, pairs[1, 1], XA, x_last[1], T - XA - XBG, T - XA)
+        gather(1, 1, 0, C)
+        quantize_x(1, 0, C)
+
+        units = [(e, m) for e in range(E) for m in range(M)]
+
+        def stage_interleave(i):
+            if 0 <= i < len(units):
+                e, m = units[i]
+                for g in range(G):
+                    interleave(e, g, m)
+
+        def stage_multiply(i):
+            if 0 <= i < len(units):
+                e, m = units[i]
+                quantize_w(e, m)
+                for g in range(G):
+                    multiply(e, g, m)
+                activate(e, m)
+
+        def stage_scatter(i):
+            if 0 <= i < len(units):
+                e, m = units[i]
+                scatter(e, m)
+                if e == E - 1:
+                    nc.sync.dma_start(out[m * P : (m + 1) * P, :], window[m][:])
+
+        stage_interleave(0)
+        stage_interleave(1)
+        stage_multiply(0)
+        gather(1, 1, C, S)
+        quantize_x(1, C, S)
+        for i in range(len(units)):
+            stage_interleave(i + 2)
+            stage_multiply(i + 1)
+            stage_scatter(i)

@@ -21,19 +21,21 @@ ADD = mybir.AluOpType.add
 P = 128
 G = K // (4 * P)
 M = N // P
+U = E * M
 XG = 448
 XA = 768
 XAG = 336
 XBG = 112
-XBV = 0
 LAST = ((0, XA), (XA, T))
+RAW_BYTES = G * 4 * P * 4
+SPLIT_UNITS = 3
+AHEAD = 2
 
-PIECES = {
-    (0, 0): ((0, 128), (128, 256), (256, 384), (384, 512)),
-    (0, 1): ((0, 128), (128, 256), (256, 384), (384, 512)),
-    (1, 0): ((0, 512),),
-    (1, 1): ((0, 256), (256, 512)),
-}
+
+def Y_OFFSET(i):
+    if i + AHEAD < U:
+        return (i + AHEAD) * RAW_BYTES
+    return U * RAW_BYTES + (i + AHEAD - U) * C * 4
 
 
 def tile_routed_moe_kernel(tc, xT, w, b, gate, offs, out):
@@ -41,43 +43,19 @@ def tile_routed_moe_kernel(tc, xT, w, b, gate, offs, out):
     with ExitStack() as ctx:
         lists = ctx.enter_context(tc.tile_pool(name="lists", bufs=1))
         keep = ctx.enter_context(tc.tile_pool(name="keep", bufs=1))
+        shared = ctx.enter_context(tc.tile_pool(name="shared", bufs=1))
         psum = ctx.enter_context(tc.psum_pool(name="psum", bufs=1))
 
         def gpsimd_copy(out, in_):
             nc.gpsimd.tensor_scalar(out=out, in0=in_, scalar1=1.0, scalar2=0.0, op0=MULT, op1=ADD)
 
-        IL = {
-            (0, 0, 0): nc.scalar.copy,
-            (0, 0, 1): nc.scalar.copy,
-            (0, 0, 2): nc.scalar.copy,
-            (0, 0, 3): nc.scalar.copy,
-            (0, 1, 0): gpsimd_copy,
-            (0, 1, 1): gpsimd_copy,
-            (0, 1, 2): nc.scalar.copy,
-            (0, 1, 3): nc.scalar.copy,
-            (1, 0, 0): nc.scalar.copy,
-            (1, 0, 1): nc.scalar.copy,
-            (1, 0, 2): nc.scalar.copy,
-            (1, 0, 3): nc.scalar.copy,
-            (1, 1, 0): nc.scalar.copy,
-            (1, 1, 1): nc.scalar.copy,
-            (1, 1, 2): nc.scalar.copy,
-            (1, 1, 3): nc.scalar.copy,
-        }
+        units = [(e, m) for e in range(E) for m in range(M)]
 
         offsets = lists.tile([P, S // 16], U16, name="offsets")
         nc.sync.dma_start(offsets[:], offs)
 
         bias = keep.tile([P, M, E], F32, name="bias")
         nc.scalar.dma_start(bias[:], b.rearrange("(m p) e -> p m e", p=P))
-
-        w_view = w.rearrange("e (g p j) n -> e g p j n", p=P, j=4)
-        w_raw = {}
-
-        def load_w(e, g, i):
-            c0, c1 = PIECES[e, g][i]
-            w_raw[e, g, i] = keep.tile([P, 4, c1 - c0], F32, name="w_raw%d%d%d" % (e, g, i))
-            nc.sync.dma_start(w_raw[e, g, i][:], w_view[e, g, :, :, c0:c1])
 
         x_view = xT.rearrange("(g p t) n -> g p t n", p=P, t=4)
         x_raw = {}
@@ -92,24 +70,27 @@ def tile_routed_moe_kernel(tc, xT, w, b, gate, offs, out):
             x_last[h] = keep.tile([P, 2, n1 - n0], F32, name="x_last%d" % h)
             nc.sync.dma_start(x_last[h][:], x_view[1, :, 2:4, n0:n1])
 
+        w_view = w.rearrange("e (g p j) n -> e g p j n", p=P, j=4)
+        w_raw = []
+
+        def load_w(i):
+            e, m = units[i]
+            w_raw.append(shared.tile([P, G, 4, P], F32, name="w_raw%d" % i, offset=i * RAW_BYTES))
+            for g in range(G):
+                nc.sync.dma_start(w_raw[i][:, g, :, :], w_view[e, g, :, :, m * P : (m + 1) * P])
+
         gate_sb = keep.tile([P, S], F32, name="gate_sb")
         load_x(0, 0)
         load_x(0, 1)
         load_x(1, 0)
         load_x_last(0)
         load_x_last(1)
-        load_w(0, 0, 0)
-        load_w(0, 1, 0)
-        load_w(0, 0, 1)
-        load_w(0, 1, 1)
+        load_w(0)
+        load_w(1)
+        load_w(2)
         nc.sync.dma_start(gate_sb[:], gate[0:P, :])
-        load_w(0, 0, 2)
-        load_w(0, 1, 2)
-        load_w(0, 0, 3)
-        load_w(0, 1, 3)
-        load_w(1, 0, 0)
-        load_w(1, 1, 0)
-        load_w(1, 1, 1)
+        for i in range(3, U):
+            load_w(i)
 
         warm_in = keep.tile([P, 1], F32, name="warm_in")
         warm_out = keep.tile([P, 1], F32, name="warm_out")
@@ -120,33 +101,31 @@ def tile_routed_moe_kernel(tc, xT, w, b, gate, offs, out):
             window.append(keep.tile([P, T], F32, name="window%d" % m))
             nc.vector.memset(window[m][:], 0.0)
 
-        w_grouped = {}
-        w_codes = {}
-        w_scales = {}
-        acc = {}
-        y = {}
-        for e in range(E):
-            for m in range(M):
-                w_grouped[e, m] = keep.tile([P, G, P, 4], BF16, name="w_grouped%d%d" % (e, m), align_bytes=64)
-                w_codes[e, m] = keep.tile([P, G * P], U32, name="w_codes%d%d" % (e, m), align_bytes=64)
-                w_scales[e, m] = keep.tile([P, G * P], U8, name="w_scales%d%d" % (e, m), align_bytes=64)
-                acc[e, m] = psum.tile([P, C], F32, name="acc%d%d" % (e, m))
-                y[e, m] = keep.tile([P, C], F32, name="y%d%d" % (e, m))
+        w_grouped = []
+        w_codes = []
+        w_scales = []
+        acc = []
+        y = []
+        for i in range(U):
+            w_grouped.append(keep.tile([P, G, P, 4], BF16, name="w_grouped%d" % i, align_bytes=64))
+            w_codes.append(keep.tile([P, G * P], U32, name="w_codes%d" % i, align_bytes=64))
+            w_scales.append(keep.tile([P, G * P], U8, name="w_scales%d" % i, align_bytes=64))
+            acc.append(psum.tile([P, C], F32, name="acc%d" % i))
 
-        def interleave(e, g, m):
-            for i, (c0, c1) in enumerate(PIECES[e, g]):
-                if c0 <= m * P < c1:
-                    a = m * P - c0
-                    IL[e, g, m](
-                        out=w_grouped[e, m][:, g, :, :],
-                        in_=w_raw[e, g, i][:, :, a : a + P].rearrange("p j n -> p n j"),
-                    )
+        def interleave(i):
+            if i >= U:
+                return
+            if i < SPLIT_UNITS:
+                nc.scalar.copy(out=w_grouped[i][:, 0, :, :], in_=w_raw[i][:, 0, :, :].rearrange("p j n -> p n j"))
+                gpsimd_copy(out=w_grouped[i][:, 1, :, :], in_=w_raw[i][:, 1, :, :].rearrange("p j n -> p n j"))
+            else:
+                nc.scalar.copy(out=w_grouped[i][:], in_=w_raw[i][:].rearrange("p g j n -> p g n j"))
 
-        def quantize_w(e, m):
+        def quantize_w(i):
             nc.vector.quantize_mx(
-                out=w_codes[e, m][:].bitcast(FP8X4),
-                scales=w_scales[e, m][:],
-                in_=w_grouped[e, m][:].rearrange("p g n j -> p (g n j)"),
+                out=w_codes[i][:].bitcast(FP8X4),
+                scales=w_scales[i][:],
+                in_=w_grouped[i][:].rearrange("p g n j -> p (g n j)"),
             )
 
         x_grouped = {}
@@ -175,27 +154,35 @@ def tile_routed_moe_kernel(tc, xT, w, b, gate, offs, out):
                 out=x_words[g][:, s0:s1, u], in_=pair_words.indirect(offsets[:, s0 // 16 : s1 // 16])
             )
 
-        def multiply(e, g, m):
-            nc.tensor.matmul_mx(
-                out=acc[e, m][:],
-                lhsT=w_codes[e, m][:, g * P : (g + 1) * P].bitcast(FP8X4),
-                lhsT_scale=w_scales[e, m][:, g * P : (g + 1) * P],
-                rhs=x_codes[g][:, e * C : (e + 1) * C].bitcast(FP8X4),
-                rhs_scale=x_scales[g][:, e * C : (e + 1) * C],
-                start=(g == 0),
-                stop=(g == G - 1),
-            )
+        def multiply(i):
+            if i >= U:
+                return
+            e, m = units[i]
+            quantize_w(i)
+            for g in range(G):
+                nc.tensor.matmul_mx(
+                    out=acc[i][:],
+                    lhsT=w_codes[i][:, g * P : (g + 1) * P].bitcast(FP8X4),
+                    lhsT_scale=w_scales[i][:, g * P : (g + 1) * P],
+                    rhs=x_codes[g][:, e * C : (e + 1) * C].bitcast(FP8X4),
+                    rhs_scale=x_scales[g][:, e * C : (e + 1) * C],
+                    start=(g == 0),
+                    stop=(g == G - 1),
+                )
 
-        def activate(e, m):
-            nc.scalar.activation(
-                out=y[e, m][:], in_=acc[e, m][:], func=GELU, bias=bias[:, m, e : e + 1], scale=1.0
-            )
+        def activate(i):
+            e, m = units[i]
+            y.append(shared.tile([P, C], F32, name="y%d" % i, offset=Y_OFFSET(i)))
+            nc.scalar.activation(out=y[i][:], in_=acc[i][:], func=GELU, bias=bias[:, m, e : e + 1], scale=1.0)
 
-        def scatter(e, m):
+        def scatter(i):
+            e, m = units[i]
             slot_offsets = offsets[:, e * (C // 16) : (e + 1) * (C // 16)]
             nc.vector.tensor_tensor(
-                out=window[m][:].indirect(slot_offsets), in0=y[e, m][:], in1=gate_sb[:, e * C : (e + 1) * C], op=MULT
+                out=window[m][:].indirect(slot_offsets), in0=y[i][:], in1=gate_sb[:, e * C : (e + 1) * C], op=MULT
             )
+            if e == E - 1:
+                nc.sync.dma_start(out[m * P : (m + 1) * P, :], window[m][:])
 
         def cast(copy, dst, n0, raw, r0, r1):
             if r1 > r0:
@@ -211,41 +198,19 @@ def tile_routed_moe_kernel(tc, xT, w, b, gate, offs, out):
         pairs[1, 1] = keep.tile([P, T, 2], BF16, name="pairs11")
         cast(nc.scalar.copy, pairs[1, 1], 0, x_last[0], 0, XA - XAG)
         cast(gpsimd_copy, pairs[1, 1], 0, x_last[0], XA - XAG, XA)
-        cast(nc.vector.tensor_copy, pairs[1, 1], XA, x_last[1], 0, XBV)
-        cast(nc.scalar.copy, pairs[1, 1], XA, x_last[1], XBV, T - XA - XBG)
+        cast(nc.scalar.copy, pairs[1, 1], XA, x_last[1], 0, T - XA - XBG)
         cast(gpsimd_copy, pairs[1, 1], XA, x_last[1], T - XA - XBG, T - XA)
         gather(1, 1, 0, C)
         quantize_x(1, 0, C)
 
-        units = [(e, m) for e in range(E) for m in range(M)]
-
-        def stage_interleave(i):
-            if 0 <= i < len(units):
-                e, m = units[i]
-                for g in range(G):
-                    interleave(e, g, m)
-
-        def stage_multiply(i):
-            if 0 <= i < len(units):
-                e, m = units[i]
-                quantize_w(e, m)
-                for g in range(G):
-                    multiply(e, g, m)
-                activate(e, m)
-
-        def stage_scatter(i):
-            if 0 <= i < len(units):
-                e, m = units[i]
-                scatter(e, m)
-                if e == E - 1:
-                    nc.sync.dma_start(out[m * P : (m + 1) * P, :], window[m][:])
-
-        stage_interleave(0)
-        stage_interleave(1)
-        stage_multiply(0)
+        interleave(0)
+        multiply(0)
         gather(1, 1, C, S)
         quantize_x(1, C, S)
-        for i in range(len(units)):
-            stage_interleave(i + 2)
-            stage_multiply(i + 1)
-            stage_scatter(i)
+        interleave(1)
+        multiply(1)
+        for i in range(U):
+            interleave(i + 2)
+            multiply(i + 2)
+            activate(i)
+            scatter(i)

@@ -29,7 +29,7 @@ XBG = 112
 LAST = ((0, XA), (XA, T))
 RAW_BYTES = G * 4 * P * 4
 SPLIT_UNITS = 3
-AHEAD = 2
+AHEAD = 1
 
 
 def Y_OFFSET(i):
@@ -207,10 +207,8 @@ def tile_routed_moe_kernel(tc, xT, w, b, gate, offs, out):
         multiply(0)
         gather(1, 1, C, S)
         quantize_x(1, C, S)
-        interleave(1)
-        multiply(1)
         for i in range(U):
-            interleave(i + 2)
-            multiply(i + 2)
+            interleave(i + 1)
+            multiply(i + 1)
             activate(i)
             scatter(i)

@@ -116,10 +116,16 @@ def tile_routed_moe_kernel(tc, xT, w, b, gate, offs, out):
             if i >= U:
                 return
             if i < SPLIT_UNITS:
-                nc.scalar.copy(out=w_grouped[i][:, 0, :, :], in_=w_raw[i][:, 0, :, :].rearrange("p j n -> p n j"))
+                nc.scalar.copy(
+                    out=w_grouped[i][:, 0, :, :].rearrange("p (c i) j -> p c j i", i=4),
+                    in_=w_raw[i][:, 0, :, :].rearrange("p j (c i) -> p c j i", i=4),
+                )
                 gpsimd_copy(out=w_grouped[i][:, 1, :, :], in_=w_raw[i][:, 1, :, :].rearrange("p j n -> p n j"))
             else:
-                nc.scalar.copy(out=w_grouped[i][:], in_=w_raw[i][:].rearrange("p g j n -> p g n j"))
+                nc.scalar.copy(
+                    out=w_grouped[i][:].rearrange("p g (c i) j -> p g c j i", i=4),
+                    in_=w_raw[i][:].rearrange("p g j (c i) -> p g c j i", i=4),
+                )
 
         def quantize_w(i):
             nc.vector.quantize_mx(

@@ -79,7 +79,12 @@ def tile_routed_moe_kernel(tc, xT, w, b, gate, offs, out):
             for g in range(G):
                 nc.sync.dma_start(w_raw[i][:, g, :, :], w_view[e, g, :, :, m * P : (m + 1) * P])
 
-        gate_sb = keep.tile([P, S], F32, name="gate_sb")
+        gate_sb = []
+
+        def load_gate(e):
+            gate_sb.append(keep.tile([P, C], F32, name="gate_sb%d" % e))
+            nc.sync.dma_start(gate_sb[e][:], gate[0:P, e * C : (e + 1) * C])
+
         load_x(0, 0)
         load_x(0, 1)
         load_x(1, 0)
@@ -87,9 +92,12 @@ def tile_routed_moe_kernel(tc, xT, w, b, gate, offs, out):
         load_x_last(1)
         load_w(0)
         load_w(1)
+        load_gate(0)
         load_w(2)
-        nc.sync.dma_start(gate_sb[:], gate[0:P, :])
-        for i in range(3, U):
+        load_w(3)
+        load_w(4)
+        load_gate(1)
+        for i in range(5, U):
             load_w(i)
 
         warm_in = keep.tile([P, 1], F32, name="warm_in")
@@ -185,7 +193,7 @@ def tile_routed_moe_kernel(tc, xT, w, b, gate, offs, out):
             e, m = units[i]
             slot_offsets = offsets[:, e * (C // 16) : (e + 1) * (C // 16)]
             nc.vector.tensor_tensor(
-                out=window[m][:].indirect(slot_offsets), in0=y[i][:], in1=gate_sb[:, e * C : (e + 1) * C], op=MULT
+                out=window[m][:].indirect(slot_offsets), in0=y[i][:], in1=gate_sb[e][:], op=MULT
             )
             if e == E - 1:
                 nc.sync.dma_start(out[m * P : (m + 1) * P, :], window[m][:])

@@ -55,7 +55,6 @@ def tile_routed_moe_kernel(tc, xT, w, b, gate, offs, out):
         nc.sync.dma_start(offsets[:], offs)
 
         bias = keep.tile([P, M, E], F32, name="bias")
-        nc.scalar.dma_start(bias[:], b.rearrange("(m p) e -> p m e", p=P))
 
         x_view = xT.rearrange("(g p t) n -> g p t n", p=P, t=4)
         x_raw = {}
@@ -90,6 +89,7 @@ def tile_routed_moe_kernel(tc, xT, w, b, gate, offs, out):
         load_x(1, 0)
         load_x_last(0)
         load_x_last(1)
+        nc.sync.dma_start(bias[:], b.rearrange("(m p) e -> p m e", p=P))
         load_w(0)
         load_w(1)
         load_gate(0)

@@ -128,7 +128,10 @@ def tile_routed_moe_kernel(tc, xT, w, b, gate, offs, out):
                     out=w_grouped[i][:, 0, :, :].rearrange("p (c i) j -> p c j i", i=4),
                     in_=w_raw[i][:, 0, :, :].rearrange("p j (c i) -> p c j i", i=4),
                 )
-                gpsimd_copy(out=w_grouped[i][:, 1, :, :], in_=w_raw[i][:, 1, :, :].rearrange("p j n -> p n j"))
+                nc.scalar.copy(
+                    out=w_grouped[i][:, 1, :, :].rearrange("p (c i) j -> p c j i", i=4),
+                    in_=w_raw[i][:, 1, :, :].rearrange("p j (c i) -> p c j i", i=4),
+                )
             else:
                 nc.scalar.copy(
                     out=w_grouped[i][:].rearrange("p g (c i) j -> p g c j i", i=4),

@@ -28,7 +28,7 @@ XAG = 336
 XBG = 112
 LAST = ((0, XA), (XA, T))
 RAW_BYTES = G * 4 * P * 4
-SPLIT_UNITS = 3
+SPLIT_UNITS = 8
 AHEAD = 1
 
 

@@ -22,7 +22,7 @@ P = 128
 G = K // (4 * P)
 M = N // P
 U = E * M
-XG = 448
+XG = {(0, 0): 448, (0, 1): 448, (1, 0): 320}
 XA = 768
 XAG = 336
 XBG = 112
@@ -52,7 +52,6 @@ def tile_routed_moe_kernel(tc, xT, w, b, gate, offs, out):
         units = [(e, m) for e in range(E) for m in range(M)]
 
         offsets = lists.tile([P, S // 16], U16, name="offsets")
-        nc.sync.dma_start(offsets[:], offs)
 
         bias = keep.tile([P, M, E], F32, name="bias")
 
@@ -85,12 +84,13 @@ def tile_routed_moe_kernel(tc, xT, w, b, gate, offs, out):
             nc.sync.dma_start(gate_sb[e][:], gate[0:P, e * C : (e + 1) * C])
 
         load_x(0, 0)
+        nc.sync.dma_start(offsets[:], offs)
         load_x(0, 1)
         load_x(1, 0)
         load_x_last(0)
         load_x_last(1)
-        nc.sync.dma_start(bias[:], b.rearrange("(m p) e -> p m e", p=P))
         load_w(0)
+        nc.sync.dma_start(bias[:], b.rearrange("(m p) e -> p m e", p=P))
         load_w(1)
         load_gate(0)
         load_w(2)
@@ -207,8 +207,8 @@ def tile_routed_moe_kernel(tc, xT, w, b, gate, offs, out):
 
         for g, u in ((0, 0), (0, 1), (1, 0)):
             pairs[g, u] = keep.tile([P, T, 2], BF16, name="pairs%d%d" % (g, u))
-            cast(nc.scalar.copy, pairs[g, u], 0, x_raw[g, u], 0, T - XG)
-            cast(gpsimd_copy, pairs[g, u], 0, x_raw[g, u], T - XG, T)
+            cast(nc.scalar.copy, pairs[g, u], 0, x_raw[g, u], 0, T - XG[g, u])
+            cast(gpsimd_copy, pairs[g, u], 0, x_raw[g, u], T - XG[g, u], T)
             gather(g, u, 0, S)
             if (g, u) == (0, 1):
                 quantize_x(0, 0, S)

@@ -22,11 +22,12 @@ P = 128
 G = K // (4 * P)
 M = N // P
 U = E * M
-XG = {(0, 0): 448, (0, 1): 448, (1, 0): 320}
-XA = 768
-XAG = 336
-XBG = 112
-LAST = ((0, XA), (XA, T))
+X_PIECES = {
+    (0, 0): ((0, 1024, 448),),
+    (0, 1): ((0, 1024, 448),),
+    (1, 0): ((0, 512, 160), (512, 1024, 160)),
+    (1, 1): ((0, 640, 288), (640, 1024, 176)),
+}
 RAW_BYTES = G * 4 * P * 4
 SPLIT_UNITS = 8
 AHEAD = 1
@@ -57,16 +58,11 @@ def tile_routed_moe_kernel(tc, xT, w, b, gate, offs, out):
 
         x_view = xT.rearrange("(g p t) n -> g p t n", p=P, t=4)
         x_raw = {}
-        x_last = {}
 
         def load_x(g, u):
-            x_raw[g, u] = keep.tile([P, 2, T], F32, name="x_raw%d%d" % (g, u))
-            nc.sync.dma_start(x_raw[g, u][:], x_view[g, :, 2 * u : 2 * u + 2, :])
-
-        def load_x_last(h):
-            n0, n1 = LAST[h]
-            x_last[h] = keep.tile([P, 2, n1 - n0], F32, name="x_last%d" % h)
-            nc.sync.dma_start(x_last[h][:], x_view[1, :, 2:4, n0:n1])
+            for n0, n1, share in X_PIECES[g, u]:
+                x_raw[g, u, n0] = keep.tile([P, 2, n1 - n0], F32, name="x_raw%d%d_%d" % (g, u, n0))
+                nc.sync.dma_start(x_raw[g, u, n0][:], x_view[g, :, 2 * u : 2 * u + 2, n0:n1])
 
         w_view = w.rearrange("e (g p j) n -> e g p j n", p=P, j=4)
         w_raw = []
@@ -87,8 +83,7 @@ def tile_routed_moe_kernel(tc, xT, w, b, gate, offs, out):
         nc.sync.dma_start(offsets[:], offs)
         load_x(0, 1)
         load_x(1, 0)
-        load_x_last(0)
-        load_x_last(1)
+        load_x(1, 1)
         load_w(0)
         nc.sync.dma_start(bias[:], b.rearrange("(m p) e -> p m e", p=P))
         load_w(1)
@@ -205,18 +200,15 @@ def tile_routed_moe_kernel(tc, xT, w, b, gate, offs, out):
             if r1 > r0:
                 copy(out=dst[:, n0 + r0 : n0 + r1, :], in_=raw[:, :, r0:r1].rearrange("p e n -> p n e"))
 
-        for g, u in ((0, 0), (0, 1), (1, 0)):
+        for g, u in ((0, 0), (0, 1), (1, 0), (1, 1)):
             pairs[g, u] = keep.tile([P, T, 2], BF16, name="pairs%d%d" % (g, u))
-            cast(nc.scalar.copy, pairs[g, u], 0, x_raw[g, u], 0, T - XG[g, u])
-            cast(gpsimd_copy, pairs[g, u], 0, x_raw[g, u], T - XG[g, u], T)
-            gather(g, u, 0, S)
+            for n0, n1, share in X_PIECES[g, u]:
+                cast(nc.scalar.copy, pairs[g, u], n0, x_raw[g, u, n0], 0, n1 - n0 - share)
+                cast(gpsimd_copy, pairs[g, u], n0, x_raw[g, u, n0], n1 - n0 - share, n1 - n0)
+            if (g, u) != (1, 1):
+                gather(g, u, 0, S)
             if (g, u) == (0, 1):
                 quantize_x(0, 0, S)
-        pairs[1, 1] = keep.tile([P, T, 2], BF16, name="pairs11")
-        cast(nc.scalar.copy, pairs[1, 1], 0, x_last[0], 0, XA - XAG)
-        cast(gpsimd_copy, pairs[1, 1], 0, x_last[0], XA - XAG, XA)
-        cast(nc.scalar.copy, pairs[1, 1], XA, x_last[1], 0, T - XA - XBG)
-        cast(gpsimd_copy, pairs[1, 1], XA, x_last[1], T - XA - XBG, T - XA)
         gather(1, 1, 0, C)
         quantize_x(1, 0, C)
 

@@ -29,7 +29,6 @@ X_PIECES = {
     (1, 1): ((0, 640, 288), (640, 1024, 176)),
 }
 RAW_BYTES = G * 4 * P * 4
-SPLIT_UNITS = 8
 AHEAD = 1
 
 
@@ -45,6 +44,7 @@ def tile_routed_moe_kernel(tc, xT, w, b, gate, offs, out):
         lists = ctx.enter_context(tc.tile_pool(name="lists", bufs=1))
         keep = ctx.enter_context(tc.tile_pool(name="keep", bufs=1))
         shared = ctx.enter_context(tc.tile_pool(name="shared", bufs=1))
+        turns = ctx.enter_context(tc.tile_pool(name="turns", bufs=1))
         psum = ctx.enter_context(tc.psum_pool(name="psum", bufs=1))
 
         def gpsimd_copy(out, in_):
@@ -110,7 +110,10 @@ def tile_routed_moe_kernel(tc, xT, w, b, gate, offs, out):
         acc = []
         y = []
         for i in range(U):
-            w_grouped.append(keep.tile([P, G, P, 4], BF16, name="w_grouped%d" % i, align_bytes=64))
+            if i == 0:
+                w_grouped.append(turns.tile([P, G, P, 4], BF16, name="w_grouped0", align_bytes=64, offset=0))
+            else:
+                w_grouped.append(keep.tile([P, G, P, 4], BF16, name="w_grouped%d" % i, align_bytes=64))
             w_codes.append(keep.tile([P, G * P], U32, name="w_codes%d" % i, align_bytes=64))
             w_scales.append(keep.tile([P, G * P], U8, name="w_scales%d" % i, align_bytes=64))
             acc.append(psum.tile([P, C], F32, name="acc%d" % i))
@@ -118,19 +121,10 @@ def tile_routed_moe_kernel(tc, xT, w, b, gate, offs, out):
         def interleave(i):
             if i >= U:
                 return
-            if i < SPLIT_UNITS:
+            for g in range(G):
                 nc.scalar.copy(
-                    out=w_grouped[i][:, 0, :, :].rearrange("p (c i) j -> p c j i", i=4),
-                    in_=w_raw[i][:, 0, :, :].rearrange("p j (c i) -> p c j i", i=4),
-                )
-                nc.scalar.copy(
-                    out=w_grouped[i][:, 1, :, :].rearrange("p (c i) j -> p c j i", i=4),
-                    in_=w_raw[i][:, 1, :, :].rearrange("p j (c i) -> p c j i", i=4),
-                )
-            else:
-                nc.scalar.copy(
-                    out=w_grouped[i][:].rearrange("p g (c i) j -> p g c j i", i=4),
-                    in_=w_raw[i][:].rearrange("p g j (c i) -> p g c j i", i=4),
+                    out=w_grouped[i][:, g, :, :].rearrange("p (c i) j -> p c j i", i=4),
+                    in_=w_raw[i][:, g, :, :].rearrange("p j (c i) -> p c j i", i=4),
                 )
 
         def quantize_w(i):
@@ -150,15 +144,19 @@ def tile_routed_moe_kernel(tc, xT, w, b, gate, offs, out):
             x_words[g] = (
                 x_grouped[g][:].rearrange("p s t -> p (s t)").bitcast(U32).rearrange("p (s u) -> p s u", u=2)
             )
-            x_codes[g] = keep.tile([P, S], U32, name="x_codes%d" % g, align_bytes=64)
-            x_scales[g] = keep.tile([P, S], U8, name="x_scales%d" % g, align_bytes=64)
 
-        def quantize_x(g, s0, s1):
+        def quantize_x(g, e0, e1, pool, **place):
+            n = (e1 - e0) * C
+            codes = pool.tile([P, n], U32, name="x_codes%d%d" % (g, e0), align_bytes=64, **place)
+            scales = keep.tile([P, n], U8, name="x_scales%d%d" % (g, e0), align_bytes=64)
             nc.vector.quantize_mx(
-                out=x_codes[g][:, s0:s1].bitcast(FP8X4),
-                scales=x_scales[g][:, s0:s1],
-                in_=x_grouped[g][:, s0:s1, :].rearrange("p s t -> p (s t)"),
+                out=codes[:].bitcast(FP8X4),
+                scales=scales[:],
+                in_=x_grouped[g][:, e0 * C : e1 * C, :].rearrange("p s t -> p (s t)"),
             )
+            for e in range(e0, e1):
+                x_codes[g, e] = codes[:, (e - e0) * C : (e - e0 + 1) * C]
+                x_scales[g, e] = scales[:, (e - e0) * C : (e - e0 + 1) * C]
 
         def gather(g, u, s0, s1):
             pair_words = pairs[g, u][:].rearrange("p n e -> p (n e)").bitcast(U32)
@@ -176,8 +174,8 @@ def tile_routed_moe_kernel(tc, xT, w, b, gate, offs, out):
                     out=acc[i][:],
                     lhsT=w_codes[i][:, g * P : (g + 1) * P].bitcast(FP8X4),
                     lhsT_scale=w_scales[i][:, g * P : (g + 1) * P],
-                    rhs=x_codes[g][:, e * C : (e + 1) * C].bitcast(FP8X4),
-                    rhs_scale=x_scales[g][:, e * C : (e + 1) * C],
+                    rhs=x_codes[g, e].bitcast(FP8X4),
+                    rhs_scale=x_scales[g, e],
                     start=(g == 0),
                     stop=(g == G - 1),
                 )
@@ -208,14 +206,14 @@ def tile_routed_moe_kernel(tc, xT, w, b, gate, offs, out):
             if (g, u) != (1, 1):
                 gather(g, u, 0, S)
             if (g, u) == (0, 1):
-                quantize_x(0, 0, S)
+                quantize_x(0, 0, E, keep)
         gather(1, 1, 0, C)
-        quantize_x(1, 0, C)
+        quantize_x(1, 0, 1, keep)
 
         interleave(0)
         multiply(0)
         gather(1, 1, C, S)
-        quantize_x(1, C, S)
+        quantize_x(1, 1, E, turns, offset=0)
         for i in range(U):
             interleave(i + 1)
             multiply(i + 1)

@@ -1,6 +1,7 @@
 from contextlib import ExitStack
 
 import concourse.mybir as mybir
+from concourse.masks import make_identity
 
 K, T, E, C, N = 1024, 1024, 2, 256, 512
 S = E * C
@@ -54,8 +55,6 @@ def tile_routed_moe_kernel(tc, xT, w, b, gate, offs, out):
 
         offsets = lists.tile([P, S // 16], U16, name="offsets")
 
-        bias = keep.tile([P, M, E], F32, name="bias")
-
         x_view = xT.rearrange("(g p t) n -> g p t n", p=P, t=4)
         x_raw = {}
 
@@ -73,26 +72,23 @@ def tile_routed_moe_kernel(tc, xT, w, b, gate, offs, out):
             for g in range(G):
                 nc.sync.dma_start(w_raw[i][:, g, :, :], w_view[e, g, :, :, m * P : (m + 1) * P])
 
-        gate_sb = []
-
-        def load_gate(e):
-            gate_sb.append(keep.tile([P, C], F32, name="gate_sb%d" % e))
-            nc.sync.dma_start(gate_sb[e][:], gate[0:P, e * C : (e + 1) * C])
+        gate_row = []
+        for e in range(E):
+            gate_row.append(keep.tile([P, C], F32, name="gate_row%d" % e))
+            nc.gpsimd.memset(gate_row[e][:], 0.0)
+        bias_rows = keep.tile([P, P * E], F32, name="bias_rows")
+        nc.gpsimd.memset(bias_rows[:], 0.0)
 
         load_x(0, 0)
+        nc.sync.dma_start(gate_row[0][0:1, :], gate[0:1, 0:C])
+        nc.sync.dma_start(bias_rows[0:M, :], b.rearrange("(m p) e -> m (p e)", p=P))
         nc.sync.dma_start(offsets[:], offs)
         load_x(0, 1)
+        nc.sync.dma_start(gate_row[1][0:1, :], gate[0:1, C:S])
         load_x(1, 0)
         load_x(1, 1)
         load_w(0)
-        nc.sync.dma_start(bias[:], b.rearrange("(m p) e -> p m e", p=P))
-        load_w(1)
-        load_gate(0)
-        load_w(2)
-        load_w(3)
-        load_w(4)
-        load_gate(1)
-        for i in range(5, U):
+        for i in range(1, U):
             load_w(i)
 
         warm_in = keep.tile([P, 1], F32, name="warm_in")
@@ -103,6 +99,26 @@ def tile_routed_moe_kernel(tc, xT, w, b, gate, offs, out):
         for m in range(M):
             window.append(keep.tile([P, T], F32, name="window%d" % m))
             nc.vector.memset(window[m][:], 0.0)
+
+        ones = keep.tile([P, P], F32, name="ones")
+        nc.gpsimd.memset(ones[:], 1.0)
+        identity = keep.tile([P, P], F32, name="identity")
+        make_identity(nc, identity[:])
+        gate_sb = []
+        for e in range(E):
+            gate_ps = psum.tile([P, C], F32, name="gate_ps%d" % e, tag="acc%d" % (U - 3 + e))
+            nc.tensor.matmul(
+                out=gate_ps[:], lhsT=ones[:], rhs=gate_row[e][:], start=True, stop=True
+            )
+            gate_sb.append(keep.tile([P, C], F32, name="gate_sb%d" % e))
+            nc.scalar.copy(out=gate_sb[e][:], in_=gate_ps[:])
+        bias_ps = psum.tile([P, E, P], F32, name="bias_ps", tag="acc%d" % (U - 1))
+        for e in range(E):
+            nc.tensor.transpose(
+                bias_ps[:, e, :], bias_rows[:].rearrange("r (p e) -> r e p", e=E)[:, e, :], identity[:]
+            )
+        bias = keep.tile([P, E, M], F32, name="bias")
+        nc.scalar.copy(out=bias[:], in_=bias_ps[:, :, 0:M])
 
         w_grouped = []
         w_codes = []
@@ -116,7 +132,7 @@ def tile_routed_moe_kernel(tc, xT, w, b, gate, offs, out):
                 w_grouped.append(keep.tile([P, G, P, 4], BF16, name="w_grouped%d" % i, align_bytes=64))
             w_codes.append(keep.tile([P, G * P], U32, name="w_codes%d" % i, align_bytes=64))
             w_scales.append(keep.tile([P, G * P], U8, name="w_scales%d" % i, align_bytes=64))
-            acc.append(psum.tile([P, C], F32, name="acc%d" % i))
+            acc.append(psum.tile([P, C], F32, name="acc%d" % i, tag="acc%d" % i))
 
         def interleave(i):
             if i >= U:
@@ -183,7 +199,7 @@ def tile_routed_moe_kernel(tc, xT, w, b, gate, offs, out):
         def activate(i):
             e, m = units[i]
             y.append(shared.tile([P, C], F32, name="y%d" % i, offset=Y_OFFSET(i)))
-            nc.scalar.activation(out=y[i][:], in_=acc[i][:], func=GELU, bias=bias[:, m, e : e + 1], scale=1.0)
+            nc.scalar.activation(out=y[i][:], in_=acc[i][:], func=GELU, bias=bias[:, e, m : m + 1], scale=1.0)
 
         def scatter(i):
             e, m = units[i]

@@ -143,11 +143,11 @@ def tile_routed_moe_kernel(tc, xT, w, b, gate, offs, out):
                     in_=w_raw[i][:, g, :, :].rearrange("p j (c i) -> p c j i", i=4),
                 )
 
-        def quantize_w(i):
+        def quantize_w(i, g0, g1):
             nc.vector.quantize_mx(
-                out=w_codes[i][:].bitcast(FP8X4),
-                scales=w_scales[i][:],
-                in_=w_grouped[i][:].rearrange("p g n j -> p (g n j)"),
+                out=w_codes[i][:, g0 * P : g1 * P].bitcast(FP8X4),
+                scales=w_scales[i][:, g0 * P : g1 * P],
+                in_=w_grouped[i][:, g0:g1, :, :].rearrange("p g n j -> p (g n j)"),
             )
 
         x_grouped = {}
@@ -184,8 +184,11 @@ def tile_routed_moe_kernel(tc, xT, w, b, gate, offs, out):
             if i >= U:
                 return
             e, m = units[i]
-            quantize_w(i)
+            if i > 0:
+                quantize_w(i, 0, G)
             for g in range(G):
+                if i == 0:
+                    quantize_w(i, g, g + 1)
                 nc.tensor.matmul_mx(
                     out=acc[i][:],
                     lhsT=w_codes[i][:, g * P : (g + 1) * P].bitcast(FP8X4),

@@ -45,7 +45,6 @@ def tile_routed_moe_kernel(tc, xT, w, b, gate, offs, out):
         lists = ctx.enter_context(tc.tile_pool(name="lists", bufs=1))
         keep = ctx.enter_context(tc.tile_pool(name="keep", bufs=1))
         shared = ctx.enter_context(tc.tile_pool(name="shared", bufs=1))
-        turns = ctx.enter_context(tc.tile_pool(name="turns", bufs=1))
         psum = ctx.enter_context(tc.psum_pool(name="psum", bufs=1))
 
         def gpsimd_copy(out, in_):
@@ -126,10 +125,7 @@ def tile_routed_moe_kernel(tc, xT, w, b, gate, offs, out):
         acc = []
         y = []
         for i in range(U):
-            if i == 0:
-                w_grouped.append(turns.tile([P, G, P, 4], BF16, name="w_grouped0", align_bytes=64, offset=0))
-            else:
-                w_grouped.append(keep.tile([P, G, P, 4], BF16, name="w_grouped%d" % i, align_bytes=64))
+            w_grouped.append(keep.tile([P, G, P, 4], BF16, name="w_grouped%d" % i, align_bytes=64))
             w_codes.append(keep.tile([P, G * P], U32, name="w_codes%d" % i, align_bytes=64))
             w_scales.append(keep.tile([P, G * P], U8, name="w_scales%d" % i, align_bytes=64))
             acc.append(psum.tile([P, C], F32, name="acc%d" % i, tag="acc%d" % i))
@@ -161,9 +157,9 @@ def tile_routed_moe_kernel(tc, xT, w, b, gate, offs, out):
                 x_grouped[g][:].rearrange("p s t -> p (s t)").bitcast(U32).rearrange("p (s u) -> p s u", u=2)
             )
 
-        def quantize_x(g, e0, e1, pool, **place):
+        def quantize_x(g, e0, e1):
             n = (e1 - e0) * C
-            codes = pool.tile([P, n], U32, name="x_codes%d%d" % (g, e0), align_bytes=64, **place)
+            codes = keep.tile([P, n], U32, name="x_codes%d%d" % (g, e0), align_bytes=64)
             scales = keep.tile([P, n], U8, name="x_scales%d%d" % (g, e0), align_bytes=64)
             nc.vector.quantize_mx(
                 out=codes[:].bitcast(FP8X4),
@@ -225,14 +221,15 @@ def tile_routed_moe_kernel(tc, xT, w, b, gate, offs, out):
             if (g, u) != (1, 1):
                 gather(g, u, 0, S)
             if (g, u) == (0, 1):
-                quantize_x(0, 0, E, keep)
+                quantize_x(0, 0, E)
         gather(1, 1, 0, C)
-        quantize_x(1, 0, 1, keep)
+        quantize_x(1, 0, 1)
 
         interleave(0)
         multiply(0)
+        nc.vector.tensor_copy(out=x_grouped[1][:, S - 1, 2:4], in_=w_grouped[0][:, G - 1, P - 1, 2:4])
         gather(1, 1, C, S)
-        quantize_x(1, 1, E, turns, offset=0)
+        quantize_x(1, 1, E)
         for i in range(U):
             interleave(i + 1)
             multiply(i + 1)

@@ -26,7 +26,7 @@ U = E * M
 X_PIECES = {
     (0, 0): ((0, 1024, 448),),
     (0, 1): ((0, 1024, 448),),
-    (1, 0): ((0, 512, 160), (512, 1024, 160)),
+    (1, 0): ((0, 1024, 384),),
     (1, 1): ((0, 640, 288), (640, 1024, 176)),
 }
 RAW_BYTES = G * 4 * P * 4
@@ -139,11 +139,11 @@ def tile_routed_moe_kernel(tc, xT, w, b, gate, offs, out):
                     in_=w_raw[i][:, g, :, :].rearrange("p j (c i) -> p c j i", i=4),
                 )
 
-        def quantize_w(i, g0, g1):
+        def quantize_w(i):
             nc.vector.quantize_mx(
-                out=w_codes[i][:, g0 * P : g1 * P].bitcast(FP8X4),
-                scales=w_scales[i][:, g0 * P : g1 * P],
-                in_=w_grouped[i][:, g0:g1, :, :].rearrange("p g n j -> p (g n j)"),
+                out=w_codes[i][:].bitcast(FP8X4),
+                scales=w_scales[i][:],
+                in_=w_grouped[i][:].rearrange("p g n j -> p (g n j)"),
             )
 
         x_grouped = {}
@@ -180,11 +180,8 @@ def tile_routed_moe_kernel(tc, xT, w, b, gate, offs, out):
             if i >= U:
                 return
             e, m = units[i]
-            if i > 0:
-                quantize_w(i, 0, G)
+            quantize_w(i)
             for g in range(G):
-                if i == 0:
-                    quantize_w(i, g, g + 1)
                 nc.tensor.matmul_mx(
                     out=acc[i][:],
                     lhsT=w_codes[i][:, g * P : (g + 1) * P].bitcast(FP8X4),
@@ -226,8 +223,8 @@ def tile_routed_moe_kernel(tc, xT, w, b, gate, offs, out):
         quantize_x(1, 0, 1)
 
         interleave(0)
+        nc.scalar.copy(out=x_grouped[1][:, S - 1, 2:4], in_=w_grouped[0][:, G - 1, P - 1, 2:4])
         multiply(0)
-        nc.vector.tensor_copy(out=x_grouped[1][:, S - 1, 2:4], in_=w_grouped[0][:, G - 1, P - 1, 2:4])
         gather(1, 1, C, S)
         quantize_x(1, 1, E)
         for i in range(U):

@@ -134,10 +134,15 @@ def tile_routed_moe_kernel(tc, xT, w, b, gate, offs, out):
             if i >= U:
                 return
             for g in range(G):
+                n1 = P // 2 if i < 2 and g == G - 1 else P
                 nc.scalar.copy(
-                    out=w_grouped[i][:, g, :, :].rearrange("p (c i) j -> p c j i", i=4),
-                    in_=w_raw[i][:, g, :, :].rearrange("p j (c i) -> p c j i", i=4),
+                    out=w_grouped[i][:, g, 0:n1, :].rearrange("p (c i) j -> p c j i", i=4),
+                    in_=w_raw[i][:, g, :, 0:n1].rearrange("p j (c i) -> p c j i", i=4),
                 )
+                if n1 < P:
+                    gpsimd_copy(
+                        out=w_grouped[i][:, g, n1:P, :], in_=w_raw[i][:, g, :, n1:P].rearrange("p j n -> p n j")
+                    )
 
         def quantize_w(i):
             nc.vector.quantize_mx(
@@ -223,7 +228,7 @@ def tile_routed_moe_kernel(tc, xT, w, b, gate, offs, out):
         quantize_x(1, 0, 1)
 
         interleave(0)
-        nc.scalar.copy(out=x_grouped[1][:, S - 1, 2:4], in_=w_grouped[0][:, G - 1, P - 1, 2:4])
+        nc.scalar.copy(out=x_grouped[1][:, S - 1, 2:4], in_=w_grouped[0][:, G - 1, 0, 2:4])
         multiply(0)
         gather(1, 1, C, S)
         quantize_x(1, 1, E)

@@ -27,7 +27,7 @@ X_PIECES = {
     (0, 0): ((0, 1024, 448),),
     (0, 1): ((0, 1024, 448),),
     (1, 0): ((0, 1024, 384),),
-    (1, 1): ((0, 640, 288), (640, 1024, 176)),
+    (1, 1): ((0, 512, 224), (512, 1024, 224)),
 }
 RAW_BYTES = G * 4 * P * 4
 AHEAD = 1
@@ -54,13 +54,17 @@ def tile_routed_moe_kernel(tc, xT, w, b, gate, offs, out):
 
         offsets = lists.tile([P, S // 16], U16, name="offsets")
 
-        x_view = xT.rearrange("(g p t) n -> g p t n", p=P, t=4)
+        x_view = xT.rearrange("(g p u e) n -> g u p (e n)", p=P, u=2, e=2)
         x_raw = {}
 
         def load_x(g, u):
+            x_raw[g, u] = keep.tile([P, 2, T], F32, name="x_raw%d%d" % (g, u))
+            start = 0
             for n0, n1, share in X_PIECES[g, u]:
-                x_raw[g, u, n0] = keep.tile([P, 2, n1 - n0], F32, name="x_raw%d%d_%d" % (g, u, n0))
-                nc.sync.dma_start(x_raw[g, u, n0][:], x_view[g, :, 2 * u : 2 * u + 2, n0:n1])
+                nc.sync.dma_start(
+                    x_raw[g, u][:].rearrange("p e n -> p (e n)")[:, start : T + n1], x_view[g, u, :, start : T + n1]
+                )
+                start = T + n1
 
         w_view = w.rearrange("e (g p j) n -> e g p j n", p=P, j=4)
         w_raw = []
@@ -211,15 +215,14 @@ def tile_routed_moe_kernel(tc, xT, w, b, gate, offs, out):
             if e == E - 1:
                 nc.sync.dma_start(out[m * P : (m + 1) * P, :], window[m][:])
 
-        def cast(copy, dst, n0, raw, r0, r1):
-            if r1 > r0:
-                copy(out=dst[:, n0 + r0 : n0 + r1, :], in_=raw[:, :, r0:r1].rearrange("p e n -> p n e"))
+        def cast(copy, dst, raw, n0, n1):
+            copy(out=dst[:, n0:n1, :], in_=raw[:, :, n0:n1].rearrange("p e n -> p n e"))
 
         for g, u in ((0, 0), (0, 1), (1, 0), (1, 1)):
             pairs[g, u] = keep.tile([P, T, 2], BF16, name="pairs%d%d" % (g, u))
             for n0, n1, share in X_PIECES[g, u]:
-                cast(nc.scalar.copy, pairs[g, u], n0, x_raw[g, u, n0], 0, n1 - n0 - share)
-                cast(gpsimd_copy, pairs[g, u], n0, x_raw[g, u, n0], n1 - n0 - share, n1 - n0)
+                cast(nc.scalar.copy, pairs[g, u], x_raw[g, u], n0, n1 - share)
+                cast(gpsimd_copy, pairs[g, u], x_raw[g, u], n1 - share, n1)
             if (g, u) != (1, 1):
                 gather(g, u, 0, S)
             if (g, u) == (0, 1):

from contextlib import ExitStack

import concourse.mybir as mybir
from concourse.masks import make_identity

K, T, E, C, N = 1024, 1024, 2, 256, 512
S = E * C

FLOPS = 2 * K * N * S
BYTES = 4 * (K * S + E * K * N + N * E + S + N * T) + 2 * 128 * (S // 16)

F32 = mybir.dt.float32
BF16 = mybir.dt.bfloat16
U32 = mybir.dt.uint32
U16 = mybir.dt.uint16
U8 = mybir.dt.uint8
FP8X4 = mybir.dt.float8_e4m3fn_x4
GELU = mybir.ActivationFunctionType.Gelu_apprx_tanh
MULT = mybir.AluOpType.mult
ADD = mybir.AluOpType.add

P = 128
G = K // (4 * P)
M = N // P
U = E * M
X_PIECES = {
    (0, 0): ((0, 1024, 448),),
    (0, 1): ((0, 1024, 448),),
    (1, 0): ((0, 1024, 384),),
    (1, 1): ((0, 512, 224), (512, 1024, 224)),
}
RAW_BYTES = G * 4 * P * 4
AHEAD = 1


def Y_OFFSET(i):
    if i + AHEAD < U:
        return (i + AHEAD) * RAW_BYTES
    return U * RAW_BYTES + (i + AHEAD - U) * C * 4


def tile_routed_moe_kernel(tc, xT, w, b, gate, offs, out):
    nc = tc.nc
    with ExitStack() as ctx:
        lists = ctx.enter_context(tc.tile_pool(name="lists", bufs=1))
        keep = ctx.enter_context(tc.tile_pool(name="keep", bufs=1))
        shared = ctx.enter_context(tc.tile_pool(name="shared", bufs=1))
        psum = ctx.enter_context(tc.psum_pool(name="psum", bufs=1))

        def gpsimd_copy(out, in_):
            nc.gpsimd.tensor_scalar(out=out, in0=in_, scalar1=1.0, scalar2=0.0, op0=MULT, op1=ADD)

        units = [(e, m) for e in range(E) for m in range(M)]

        offsets = lists.tile([P, S // 16], U16, name="offsets")

        x_view = xT.rearrange("(g p u e) n -> g u p (e n)", p=P, u=2, e=2)
        x_raw = {}

        def load_x(g, u):
            x_raw[g, u] = keep.tile([P, 2, T], F32, name="x_raw%d%d" % (g, u))
            start = 0
            for n0, n1, share in X_PIECES[g, u]:
                nc.sync.dma_start(
                    x_raw[g, u][:].rearrange("p e n -> p (e n)")[:, start : T + n1], x_view[g, u, :, start : T + n1]
                )
                start = T + n1

        w_view = w.rearrange("e (g p j) n -> e g p j n", p=P, j=4)
        w_raw = []

        def load_w(i):
            e, m = units[i]
            w_raw.append(shared.tile([P, G, 4, P], F32, name="w_raw%d" % i, offset=i * RAW_BYTES))
            for g in range(G):
                nc.sync.dma_start(w_raw[i][:, g, :, :], w_view[e, g, :, :, m * P : (m + 1) * P])

        gate_row = []
        for e in range(E):
            gate_row.append(keep.tile([P, C], F32, name="gate_row%d" % e))
            nc.gpsimd.memset(gate_row[e][:], 0.0)
        bias_rows = keep.tile([P, P * E], F32, name="bias_rows")
        nc.gpsimd.memset(bias_rows[:], 0.0)

        load_x(0, 0)
        nc.sync.dma_start(gate_row[0][0:1, :], gate[0:1, 0:C])
        nc.sync.dma_start(bias_rows[0:M, :], b.rearrange("(m p) e -> m (p e)", p=P))
        nc.sync.dma_start(offsets[:], offs)
        load_x(0, 1)
        nc.sync.dma_start(gate_row[1][0:1, :], gate[0:1, C:S])
        load_x(1, 0)
        load_x(1, 1)
        load_w(0)
        for i in range(1, U):
            load_w(i)

        warm_in = keep.tile([P, 1], F32, name="warm_in")
        warm_out = keep.tile([P, 1], F32, name="warm_out")
        nc.vector.memset(warm_in[:], 0.0)
        nc.scalar.activation(out=warm_out[:], in_=warm_in[:], func=GELU)
        window = []
        for m in range(M):
            window.append(keep.tile([P, T], F32, name="window%d" % m))
            nc.vector.memset(window[m][:], 0.0)

        ones = keep.tile([P, P], F32, name="ones")
        nc.gpsimd.memset(ones[:], 1.0)
        identity = keep.tile([P, P], F32, name="identity")
        make_identity(nc, identity[:])
        gate_sb = []
        for e in range(E):
            gate_ps = psum.tile([P, C], F32, name="gate_ps%d" % e, tag="acc%d" % (U - 3 + e))
            nc.tensor.matmul(
                out=gate_ps[:], lhsT=ones[:], rhs=gate_row[e][:], start=True, stop=True
            )
            gate_sb.append(keep.tile([P, C], F32, name="gate_sb%d" % e))
            nc.scalar.copy(out=gate_sb[e][:], in_=gate_ps[:])
        bias_ps = psum.tile([P, E, P], F32, name="bias_ps", tag="acc%d" % (U - 1))
        for e in range(E):
            nc.tensor.transpose(
                bias_ps[:, e, :], bias_rows[:].rearrange("r (p e) -> r e p", e=E)[:, e, :], identity[:]
            )
        bias = keep.tile([P, E, M], F32, name="bias")
        nc.scalar.copy(out=bias[:], in_=bias_ps[:, :, 0:M])

        w_grouped = []
        w_codes = []
        w_scales = []
        acc = []
        y = []
        for i in range(U):
            w_grouped.append(keep.tile([P, G, P, 4], BF16, name="w_grouped%d" % i, align_bytes=64))
            w_codes.append(keep.tile([P, G * P], U32, name="w_codes%d" % i, align_bytes=64))
            w_scales.append(keep.tile([P, G * P], U8, name="w_scales%d" % i, align_bytes=64))
            acc.append(psum.tile([P, C], F32, name="acc%d" % i, tag="acc%d" % i))

        def interleave(i):
            if i >= U:
                return
            for g in range(G):
                n1 = P // 2 if i < 2 and g == G - 1 else P
                nc.scalar.copy(
                    out=w_grouped[i][:, g, 0:n1, :].rearrange("p (c i) j -> p c j i", i=4),
                    in_=w_raw[i][:, g, :, 0:n1].rearrange("p j (c i) -> p c j i", i=4),
                )
                if n1 < P:
                    gpsimd_copy(
                        out=w_grouped[i][:, g, n1:P, :], in_=w_raw[i][:, g, :, n1:P].rearrange("p j n -> p n j")
                    )

        def quantize_w(i):
            nc.vector.quantize_mx(
                out=w_codes[i][:].bitcast(FP8X4),
                scales=w_scales[i][:],
                in_=w_grouped[i][:].rearrange("p g n j -> p (g n j)"),
            )

        x_grouped = {}
        x_words = {}
        x_codes = {}
        x_scales = {}
        pairs = {}
        for g in range(G):
            x_grouped[g] = keep.tile([P, S, 4], BF16, name="x_grouped%d" % g, align_bytes=64)
            x_words[g] = (
                x_grouped[g][:].rearrange("p s t -> p (s t)").bitcast(U32).rearrange("p (s u) -> p s u", u=2)
            )

        def quantize_x(g, e0, e1):
            n = (e1 - e0) * C
            codes = keep.tile([P, n], U32, name="x_codes%d%d" % (g, e0), align_bytes=64)
            scales = keep.tile([P, n], U8, name="x_scales%d%d" % (g, e0), align_bytes=64)
            nc.vector.quantize_mx(
                out=codes[:].bitcast(FP8X4),
                scales=scales[:],
                in_=x_grouped[g][:, e0 * C : e1 * C, :].rearrange("p s t -> p (s t)"),
            )
            for e in range(e0, e1):
                x_codes[g, e] = codes[:, (e - e0) * C : (e - e0 + 1) * C]
                x_scales[g, e] = scales[:, (e - e0) * C : (e - e0 + 1) * C]

        def gather(g, u, s0, s1):
            pair_words = pairs[g, u][:].rearrange("p n e -> p (n e)").bitcast(U32)
            nc.vector.tensor_copy(
                out=x_words[g][:, s0:s1, u], in_=pair_words.indirect(offsets[:, s0 // 16 : s1 // 16])
            )

        def multiply(i):
            if i >= U:
                return
            e, m = units[i]
            quantize_w(i)
            for g in range(G):
                nc.tensor.matmul_mx(
                    out=acc[i][:],
                    lhsT=w_codes[i][:, g * P : (g + 1) * P].bitcast(FP8X4),
                    lhsT_scale=w_scales[i][:, g * P : (g + 1) * P],
                    rhs=x_codes[g, e].bitcast(FP8X4),
                    rhs_scale=x_scales[g, e],
                    start=(g == 0),
                    stop=(g == G - 1),
                )

        def activate(i):
            e, m = units[i]
            y.append(shared.tile([P, C], F32, name="y%d" % i, offset=Y_OFFSET(i)))
            nc.scalar.activation(out=y[i][:], in_=acc[i][:], func=GELU, bias=bias[:, e, m : m + 1], scale=1.0)

        def scatter(i):
            e, m = units[i]
            slot_offsets = offsets[:, e * (C // 16) : (e + 1) * (C // 16)]
            nc.vector.tensor_tensor(
                out=window[m][:].indirect(slot_offsets), in0=y[i][:], in1=gate_sb[e][:], op=MULT
            )
            if e == E - 1:
                nc.sync.dma_start(out[m * P : (m + 1) * P, :], window[m][:])

        def cast(copy, dst, raw, n0, n1):
            copy(out=dst[:, n0:n1, :], in_=raw[:, :, n0:n1].rearrange("p e n -> p n e"))

        for g, u in ((0, 0), (0, 1), (1, 0), (1, 1)):
            pairs[g, u] = keep.tile([P, T, 2], BF16, name="pairs%d%d" % (g, u))
            for n0, n1, share in X_PIECES[g, u]:
                cast(nc.scalar.copy, pairs[g, u], x_raw[g, u], n0, n1 - share)
                cast(gpsimd_copy, pairs[g, u], x_raw[g, u], n1 - share, n1)
            if (g, u) != (1, 1):
                gather(g, u, 0, S)
            if (g, u) == (0, 1):
                quantize_x(0, 0, E)
        gather(1, 1, 0, C)
        quantize_x(1, 0, 1)

        interleave(0)
        nc.scalar.copy(out=x_grouped[1][:, S - 1, 2:4], in_=w_grouped[0][:, G - 1, 0, 2:4])
        multiply(0)
        gather(1, 1, C, S)
        quantize_x(1, 1, E)
        for i in range(U):
            interleave(i + 1)
            multiply(i + 1)
            activate(i)
            scatter(i)
